import numpy as np
import ml_dtypes


def mxq(x, axis, fmt="e4m3"):
    dtype, down = {"e4m3": (ml_dtypes.float8_e4m3fn, 7), "e5m2": (ml_dtypes.float8_e5m2, 14)}[fmt]
    v = np.moveaxis(np.asarray(x, np.float32).astype(ml_dtypes.bfloat16).astype(np.float64), axis, -1)
    blocks = v.reshape(v.shape[:-1] + (-1, 32))
    amax = np.abs(blocks).max(-1, keepdims=True)
    byte = np.maximum(np.where(amax > 0, np.frexp(amax)[1] - 1 + 127, 0) - down, 1)
    scale = np.exp2(byte - 127.0)
    codes = (blocks / scale).astype(np.float32).astype(dtype).astype(np.float64)
    return np.moveaxis((codes * scale).reshape(v.shape), -1, axis)


WIDE = False


def mx_kscale(k):
    if not WIDE:
        return np.ones(k)
    levels = np.array([10, -10, 5, -5, 0])
    if k % 512:
        return np.exp2(np.random.permutation(np.resize(levels, k // 32))).repeat(32)
    a = np.empty((k // 512, 16))
    for p in range(k // 512):
        a[p, :8] = np.random.permutation(np.resize(levels, 8))
        for g in range(8):
            far = levels[np.abs(levels - a[p, g]) >= 10]
            a[p, g + 8] = far[np.random.randint(len(far))]
    return np.exp2(a.ravel()).repeat(32)


BF16 = ml_dtypes.bfloat16


def bf(x):
    return np.asarray(x, np.float32).astype(BF16)


def f64(x):
    return np.asarray(x).astype(np.float64)


B, N, D, E, F = 2, 512, 1024, 1024, 1024


def draw0():
    s, t = mx_kscale(D), mx_kscale(E)
    return {"x": bf(np.random.standard_normal((B, N, D)) * s),
            "wi": bf(np.random.standard_normal(D) * 2.0 / np.sqrt(D) / s),
            "wk": bf(np.random.standard_normal((D, E)) * 2.0 / np.sqrt(D) / s[:, None]),
            "wv": bf(np.random.standard_normal((D, E)) / np.sqrt(D) / s[:, None] * t),
            "wo": bf(np.random.standard_normal((E, F)) / np.sqrt(E) / t[:, None]),
            "bo": bf(np.random.standard_normal(F) * 0.1)}


def context_scores(x, wi):
    a = np.sum(x * wi, axis=-1)
    e = np.exp(a - a.max(axis=1, keepdims=True))
    return e / e.sum(axis=1, keepdims=True)


def core(x, wi, wk, wv, wo, bo):
    xf = f64(x)
    c = context_scores(xf, f64(wi))
    xq = mxq(xf, 2, "e4m3")
    k = xq @ mxq(f64(wk), 0, "e4m3")
    cv = np.sum(c[:, :, None] * k, axis=1)
    v = np.maximum(xq @ mxq(f64(wv), 0, "e4m3"), 0.0)
    z = v * cv[:, None, :]
    return (mxq(z, 2, "e4m3") @ mxq(f64(wo), 0, "e4m3")) + f64(bo)


def e4m3fn_bytes(y):
    return np.clip(np.asarray(y, np.float64), -448.0, 448.0).astype(np.float32).astype(ml_dtypes.float8_e4m3fn).view(np.uint8)


def e4m3fn_values(b):
    return np.asarray(b, np.uint8).view(ml_dtypes.float8_e4m3fn).astype(np.float64)


def setup_inputs():
    d = draw0()
    x0 = np.asarray(d['wo']).astype(np.float64)
    s = (np.max(np.abs(x0), axis=(1,), keepdims=True) / 448.0).astype(np.float32)
    out = {}
    for k, v in d.items():
        if k == 'wo':
            out['wo_bytes'] = e4m3fn_bytes(x0 / s.astype(np.float64))
            out['wo_scale'] = s
        else:
            out[k] = v
    return out


def reference(x, wi, wk, wv, wo_bytes, wo_scale, bo):
    return core(x, wi, wk, wv, e4m3fn_values(wo_bytes) * wo_scale.astype(np.float64), bo)

@@ -1,0 +1,284 @@
+from contextlib import ExitStack
+
+import concourse.mybir as mybir
+from concourse.masks import make_identity
+
+B, N, D, E, F = 2, 512, 1024, 1024, 1024
+FLOPS = 2 * B * N * (D * E * 2 + E * F) + 2 * B * N * D + 2 * B * N * E
+
+F32 = mybir.dt.float32
+BF16 = mybir.dt.bfloat16
+U32 = mybir.dt.uint32
+U8 = mybir.dt.uint8
+FP8 = mybir.dt.float8_e4m3fn
+FP8X4 = mybir.dt.float8_e4m3fn_x4
+ALU = mybir.AluOpType
+ACT = mybir.ActivationFunctionType
+
+P = 128
+PACK = 4
+K_PASS = P * PACK
+PASSES = 2
+BANK = 512
+TILES = N // P
+PAIR = 2 * P
+
+
+def tile_mobilevitv2separablecontextgate_kernel(tc, x, wi, wk, wv, wo_bytes, wo_scale, bo, out):
+    nc = tc.nc
+    with ExitStack() as ctx:
+        keep = ctx.enter_context(tc.tile_pool(name="keep", bufs=1))
+        ring = ctx.enter_context(tc.tile_pool(name="ring", bufs=1))
+        psum = ctx.enter_context(tc.psum_pool(name="psum", bufs=8))
+        ctx.enter_context(tc.manual_schedule())
+
+        def kept(name, shape, dtype):
+            return keep.tile(shape, dtype, name=name, align_bytes=64)
+
+        def bank():
+            return psum.tile([P, BANK], F32, name="bank", tag="bank")
+
+        def mx_operand(name):
+            return kept(name + "_codes", [P, BANK], U32), kept(name + "_scales", [P, BANK], U8)
+
+        def quantize(operand, cols, grouped):
+            codes, scales = operand
+            nc.vector.quantize_mx(out=codes[:, cols].bitcast(FP8X4), scales=scales[:, cols], in_=grouped[:])
+
+        def mx_product(acc, stationary, s_cols, moving, m_cols):
+            for g in range(PASSES):
+                nc.tensor.matmul_mx(
+                    out=acc,
+                    lhsT=stationary[g][0][:, s_cols].bitcast(FP8X4),
+                    lhsT_scale=stationary[g][1][:, s_cols],
+                    rhs=moving[g][0][:, m_cols].bitcast(FP8X4),
+                    rhs_scale=moving[g][1][:, m_cols],
+                    start=(g == 0),
+                    stop=(g == PASSES - 1),
+                )
+
+        def load_x(b, half):
+            rows = kept("x_rows_%d%d" % (b, half), [P, 2 * D], BF16)
+            src = x[b].rearrange("(p j) d -> p j d", j=TILES)[:, 2 * half : 2 * half + 2, :]
+            nc.sync.dma_start(out=rows[:].rearrange("p (j d) -> p j d", j=2), in_=src)
+            return rows
+
+        def load_weight(name, w, g, h):
+            rows = kept("%s_rows_%d%d" % (name, g, h), [P, PACK, BANK], BF16)
+            src = w[g * K_PASS : (g + 1) * K_PASS, h * BANK : (h + 1) * BANK]
+            nc.sync.dma_start(out=rows[:], in_=src.rearrange("(p j) e -> p j e", j=PACK))
+            return rows
+
+        wi_sb = kept("wi_sb", [P, PASSES, PACK], BF16)
+        nc.sync.dma_start(out=wi_sb[:], in_=wi.rearrange("(g p t) -> p g t", p=P, t=PACK))
+        x_rows, wk_rows, wv_rows, wo_codes_in = {}, {}, {}, {}
+        x_rows[0, 0] = load_x(0, 0)
+        wk_rows[0, 0] = load_weight("wk", wk, 0, 0)
+        x_rows[0, 1] = load_x(0, 1)
+        wk_rows[1, 0] = load_weight("wk", wk, 1, 0)
+        wk_rows[0, 1] = load_weight("wk", wk, 0, 1)
+        wk_rows[1, 1] = load_weight("wk", wk, 1, 1)
+        x_rows[1, 0] = load_x(1, 0)
+        x_rows[1, 1] = load_x(1, 1)
+        for h in range(2):
+            for g in range(PASSES):
+                wv_rows[g, h] = load_weight("wv", wv, g, h)
+        wo_scale_sb = kept("wo_scale_sb", [P, PASSES, PACK], F32)
+        nc.sync.dma_start(out=wo_scale_sb[:], in_=wo_scale.rearrange("(g p t) o -> p g (t o)", p=P, t=PACK))
+        for g in range(PASSES):
+            wo_codes_in[g] = kept("wo_bytes_sb_%d" % g, [P, PACK * F], U8)
+            src = wo_bytes[g * K_PASS : (g + 1) * K_PASS, :].rearrange("(p t) f -> p (t f)", t=PACK)
+            nc.sync.dma_start(out=wo_codes_in[g][:], in_=src)
+        bias = kept("bias", [P, F], BF16)
+        nc.sync.dma_start(out=bias[:], in_=bo.partition_broadcast(P))
+
+        ident = kept("ident", [P, P], F32)
+        make_identity(nc, ident[:])
+
+        xq = {b: [mx_operand("xq_%d%d" % (b, g)) for g in range(PASSES)] for b in range(B)}
+        zq = {b: [mx_operand("zq_%d%d" % (b, g)) for g in range(PASSES)] for b in range(B)}
+        wkq = {h: [mx_operand("wkq_%d%d" % (g, h)) for g in range(PASSES)] for h in range(2)}
+        wvq = {h: [mx_operand("wvq_%d%d" % (g, h)) for g in range(PASSES)] for h in range(2)}
+        woq = {h: [mx_operand("woq_%d%d" % (g, h)) for g in range(PASSES)] for h in range(2)}
+        every = slice(0, BANK)
+        xt, scores, neg_max, expo, total, inv_total, cv, zt = {}, {}, {}, {}, {}, {}, {}, {}
+
+        def turn_x(b, half):
+            words = x_rows[b, half][:].bitcast(F32)
+            for g in range(PASSES):
+                turned = bank()
+                view = turned[:].rearrange("p (j u r) -> p j u r", j=2, u=2)
+                for j in range(2):
+                    first = j * (D // 2) + g * (K_PASS // 2)
+                    for u in range(2):
+                        nc.tensor.transpose(view[:, j, u, :], words[:, first + u : first + K_PASS // 2 : 2], ident[:])
+                xt[b, g, half] = kept("xt_%d%d%d" % (b, g, half), [P, PAIR * PACK], BF16)
+                dst = xt[b, g, half][:].bitcast(F32).rearrange("p (j r u) -> p j r u", j=2, u=2)
+                nc.scalar.copy(out=dst, in_=view.rearrange("p j u r -> p j r u"))
+
+        def quantize_x(b, half):
+            for g in range(PASSES):
+                quantize(xq[b][g], slice(half * PAIR, (half + 1) * PAIR), xt[b, g, half])
+
+        def score(b):
+            scores[b] = bank()
+            for half in range(2):
+                for g in range(PASSES):
+                    planes = xt[b, g, half][:].rearrange("p (n t) -> p n t", t=PACK)
+                    for t in range(PACK):
+                        nc.tensor.matmul(
+                            scores[b][:, half * PAIR : (half + 1) * PAIR],
+                            lhsT=wi_sb[:, g, t : t + 1].to_broadcast([P, P]),
+                            rhs=planes[:, :, t],
+                            start=(g == 0 and t == 0),
+                            stop=(g == PASSES - 1 and t == PACK - 1),
+                        )
+
+        def score_max(b):
+            neg_max[b] = kept("neg_max_%d" % b, [P, 1], F32)
+            nc.vector.tensor_reduce(
+                out=neg_max[b][:], in_=scores[b][:], axis=mybir.AxisListType.X, op=ALU.max, negate=True
+            )
+
+        def score_exp(b):
+            expo[b] = kept("expo_%d" % b, [P, N], F32)
+            total[b] = kept("total_%d" % b, [P, 1], F32)
+            nc.scalar.activation(
+                out=expo[b][:], in_=scores[b][:], func=ACT.Exp, bias=neg_max[b][:], scale=1.0, accum_out=total[b][:]
+            )
+
+        def invert_total(b):
+            inv_total[b] = kept("inv_total_%d" % b, [P, 1], F32)
+            cv[b] = kept("cv_%d" % b, [P, 2 * PACK], F32)
+            nc.vector.reciprocal(out=inv_total[b][:], in_=total[b][:])
+
+        def grouped_tile():
+            return ring.tile([P, BANK * PACK], BF16, name="grouped", tag="grouped", bufs=4, align_bytes=64)
+
+        def group_channels(copy, rows):
+            grouped = grouped_tile()
+            copy(
+                out=grouped[:].rearrange("p (t q r j) -> p q j r t", t=PACK, r=2, j=PACK),
+                in_=rows[:].rearrange("p j (q r t) -> p q j r t", r=2, t=PACK),
+            )
+            return grouped
+
+        def group_wo(g, h):
+            planes = ring.tile([P, PACK, BANK], BF16, name="planes", tag="planes", bufs=2, align_bytes=64)
+            for t in range(PACK):
+                first = t * F + h * BANK
+                nc.scalar.activation(
+                    out=planes[:, t, :],
+                    in_=wo_codes_in[g][:, first : first + BANK].bitcast(FP8),
+                    func=ACT.Copy,
+                    scale=wo_scale_sb[:, g, t : t + 1],
+                )
+            grouped = grouped_tile()
+            nc.scalar.copy(
+                out=grouped[:].rearrange("p (c i t) -> p c t i", i=4, t=PACK),
+                in_=planes[:].rearrange("p t (c i) -> p c t i", i=4),
+            )
+            return grouped
+
+        def pool_keys(b, h, slots):
+            for t in slots:
+                keys = bank()
+                mx_product(keys[:], wkq[h], slice(t * P, (t + 1) * P), xq[b], every)
+                weighted = ring.tile([P, N], F32, name="weighted", tag="weighted", bufs=2)
+                col = h * PACK + t
+                nc.vector.scalar_tensor_tensor(
+                    out=weighted[:], in0=keys[:], scalar=inv_total[b][:], in1=expo[b][:],
+                    op0=ALU.mult, op1=ALU.mult, accum_out=cv[b][:, col : col + 1],
+                )
+
+        def gate_values(b, h, tiles):
+            if (b, h) not in zt:
+                zt[b, h] = kept("zt_%d%d" % (b, h), [P, N * PACK], BF16)
+            for j in tiles:
+                values = bank()
+                for t in range(PACK):
+                    mx_product(values[:, t * P : (t + 1) * P], wvq[h], slice(t * P, (t + 1) * P), xq[b], slice(j * P, (j + 1) * P))
+                nc.vector.scalar_tensor_tensor(
+                    out=zt[b, h][:, j * BANK : (j + 1) * BANK].rearrange("p (n t) -> p n t", t=PACK),
+                    in0=values[:].rearrange("p (t n) -> p n t", t=PACK),
+                    scalar=0.0,
+                    in1=cv[b][:, h * PACK : (h + 1) * PACK].unsqueeze(1).to_broadcast([P, P, PACK]),
+                    op0=ALU.max, op1=ALU.mult,
+                )
+
+        def project(b, h, tiles):
+            cols = slice(h * BANK, (h + 1) * BANK)
+            for j in tiles:
+                acc = bank()
+                mx_product(acc[:], zq[b], slice(j * P, (j + 1) * P), woq[h], every)
+                result = ring.tile([P, BANK], F32, name="result", tag="result", bufs=8)
+                nc.vector.tensor_tensor(out=result[:], in0=acc[:], in1=bias[:, cols], op=ALU.add)
+                nc.sync.dma_start(out=out[b].rearrange("(p j) f -> p j f", j=TILES)[:, j, cols], in_=result[:])
+
+        on_vector, on_scalar = nc.vector.tensor_copy, nc.scalar.copy
+        all4 = range(4)
+
+        turn_x(0, 0)
+        g00 = group_channels(on_vector, wk_rows[0, 0])
+        quantize_x(0, 0)
+        quantize(wkq[0][0], every, g00)
+        turn_x(0, 1)
+        g10 = group_channels(on_vector, wk_rows[1, 0])
+        quantize_x(0, 1)
+        quantize(wkq[0][1], every, g10)
+        score(0)
+        g01 = group_channels(on_scalar, wk_rows[0, 1])
+        score_max(0)
+        score_exp(0)
+        g11 = group_channels(on_vector, wk_rows[1, 1])
+        invert_total(0)
+        quantize(wkq[1][0], every, g01)
+        quantize(wkq[1][1], every, g11)
+        pool_keys(0, 0, all4)
+        turn_x(1, 0)
+        turn_x(1, 1)
+        quantize_x(1, 0)
+        quantize_x(1, 1)
+        score(1)
+        score_max(1)
+        g00 = group_channels(on_scalar, wv_rows[0, 0])
+        score_exp(1)
+        pool_keys(0, 1, all4)
+        invert_total(1)
+        quantize(wvq[0][0], every, g00)
+        g10 = group_channels(on_scalar, wv_rows[1, 0])
+        pool_keys(1, 0, all4)
+        quantize(wvq[0][1], every, g10)
+        g01 = group_channels(on_scalar, wv_rows[0, 1])
+        pool_keys(1, 1, range(0, 2))
+        quantize(wvq[1][0], every, g01)
+        g11 = group_channels(on_scalar, wv_rows[1, 1])
+        pool_keys(1, 1, range(2, 4))
+        gate_values(0, 0, range(0, 2))
+        quantize(wvq[1][1], every, g11)
+        gate_values(0, 0, range(2, 4))
+        gate_values(0, 1, range(0, 1))
+        quantize(zq[0][0], every, zt[0, 0])
+        gate_values(0, 1, range(1, 4))
+        g00 = group_wo(0, 0)
+        g10 = group_wo(1, 0)
+        gate_values(1, 0, range(0, 1))
+        quantize(zq[0][1], every, zt[0, 1])
+        quantize(woq[0][0], every, g00)
+        gate_values(1, 0, range(1, 4))
+        quantize(woq[0][1], every, g10)
+        gate_values(1, 1, range(0, 1))
+        quantize(zq[1][0], every, zt[1, 0])
+        project(0, 0, range(0, 2))
+        gate_values(1, 1, range(1, 4))
+        project(0, 0, range(2, 3))
+        quantize(zq[1][1], every, zt[1, 1])
+        project(0, 0, range(3, 4))
+        g01 = group_wo(0, 1)
+        g11 = group_wo(1, 1)
+        quantize(woq[1][0], every, g01)
+        project(1, 0, range(0, 3))
+        quantize(woq[1][1], every, g11)
+        project(1, 0, range(3, 4))
+        project(0, 1, all4)
+        project(1, 1, all4)

@@ -69,26 +69,30 @@ def tile_mobilevitv2separablecontextgate_kernel(tc, x, wi, wk, wv, wo_bytes, wo_
             nc.sync.dma_start(out=rows[:], in_=src.rearrange("(p j) e -> p j e", j=PACK))
             return rows
 
-        wi_sb = kept("wi_sb", [P, PASSES, PACK], BF16)
-        nc.sync.dma_start(out=wi_sb[:], in_=wi.rearrange("(g p t) -> p g t", p=P, t=PACK))
+        def load_wo(g):
+            codes = kept("wo_bytes_sb_%d" % g, [P, PACK * F], U8)
+            src = wo_bytes[g * K_PASS : (g + 1) * K_PASS, :].rearrange("(p t) f -> p (t f)", t=PACK)
+            nc.sync.dma_start(out=codes[:], in_=src)
+            return codes
+
         x_rows, wk_rows, wv_rows, wo_codes_in = {}, {}, {}, {}
         x_rows[0, 0] = load_x(0, 0)
         wk_rows[0, 0] = load_weight("wk", wk, 0, 0)
         x_rows[0, 1] = load_x(0, 1)
+        wi_sb = kept("wi_sb", [P, PASSES, PACK], BF16)
+        nc.sync.dma_start(out=wi_sb[:], in_=wi.rearrange("(g p t) -> p g t", p=P, t=PACK))
         wk_rows[1, 0] = load_weight("wk", wk, 1, 0)
         wk_rows[0, 1] = load_weight("wk", wk, 0, 1)
         wk_rows[1, 1] = load_weight("wk", wk, 1, 1)
+        wo_scale_sb = kept("wo_scale_sb", [P, PASSES, PACK], F32)
+        nc.sync.dma_start(out=wo_scale_sb[:], in_=wo_scale.rearrange("(g p t) o -> p g (t o)", p=P, t=PACK))
+        wo_codes_in[0] = load_wo(0)
         x_rows[1, 0] = load_x(1, 0)
         x_rows[1, 1] = load_x(1, 1)
         for h in range(2):
             for g in range(PASSES):
                 wv_rows[g, h] = load_weight("wv", wv, g, h)
-        wo_scale_sb = kept("wo_scale_sb", [P, PASSES, PACK], F32)
-        nc.sync.dma_start(out=wo_scale_sb[:], in_=wo_scale.rearrange("(g p t) o -> p g (t o)", p=P, t=PACK))
-        for g in range(PASSES):
-            wo_codes_in[g] = kept("wo_bytes_sb_%d" % g, [P, PACK * F], U8)
-            src = wo_bytes[g * K_PASS : (g + 1) * K_PASS, :].rearrange("(p t) f -> p (t f)", t=PACK)
-            nc.sync.dma_start(out=wo_codes_in[g][:], in_=src)
+        wo_codes_in[1] = load_wo(1)
         bias = kept("bias", [P, F], BF16)
         nc.sync.dma_start(out=bias[:], in_=bo.partition_broadcast(P))
 
@@ -155,16 +159,27 @@ def tile_mobilevitv2separablecontextgate_kernel(tc, x, wi, wk, wv, wo_bytes, wo_
         def grouped_tile():
             return ring.tile([P, BANK * PACK], BF16, name="grouped", tag="grouped", bufs=4, align_bytes=64)
 
-        def group_channels(copy, rows):
-            grouped = grouped_tile()
+        def paced_tile():
+            return ring.tile([P, BANK * PACK], BF16, name="paced", tag="paced", bufs=1, align_bytes=64)
+
+        def group_channels(copy, rows, grouped):
             copy(
                 out=grouped[:].rearrange("p (t q r j) -> p q j r t", t=PACK, r=2, j=PACK),
                 in_=rows[:].rearrange("p j (q r t) -> p q j r t", r=2, t=PACK),
             )
             return grouped
 
-        def group_wo(g, h):
-            planes = ring.tile([P, PACK, BANK], BF16, name="planes", tag="planes", bufs=2, align_bytes=64)
+        def group_channels_on_gpsimd(rows):
+            grouped = paced_tile()
+            nc.gpsimd.tensor_scalar(
+                out=grouped[:].rearrange("p (t m j) -> p t m j", t=PACK, j=PACK),
+                in0=rows[:].rearrange("p j (m t) -> p t m j", t=PACK),
+                scalar1=1.0, scalar2=0.0, op0=ALU.mult, op1=ALU.add,
+            )
+            return grouped
+
+        def widen_wo(g, h):
+            planes = ring.tile([P, PACK, BANK], BF16, name="planes", tag="planes", bufs=3, align_bytes=64)
             for t in range(PACK):
                 first = t * F + h * BANK
                 nc.scalar.activation(
@@ -173,10 +188,22 @@ def tile_mobilevitv2separablecontextgate_kernel(tc, x, wi, wk, wv, wo_bytes, wo_
                     func=ACT.Copy,
                     scale=wo_scale_sb[:, g, t : t + 1],
                 )
+            return planes
+
+        def interleave_on_scalar(planes):
             grouped = grouped_tile()
             nc.scalar.copy(
                 out=grouped[:].rearrange("p (c i t) -> p c t i", i=4, t=PACK),
                 in_=planes[:].rearrange("p t (c i) -> p c t i", i=4),
+            )
+            return grouped
+
+        def interleave_on_gpsimd(planes):
+            grouped = paced_tile()
+            nc.gpsimd.tensor_scalar(
+                out=grouped[:].rearrange("p (n t) -> p n t", t=PACK),
+                in0=planes[:].rearrange("p t n -> p n t"),
+                scalar1=1.0, scalar2=0.0, op0=ALU.mult, op1=ALU.add,
             )
             return grouped
 
@@ -191,94 +218,96 @@ def tile_mobilevitv2separablecontextgate_kernel(tc, x, wi, wk, wv, wo_bytes, wo_
                     op0=ALU.mult, op1=ALU.mult, accum_out=cv[b][:, col : col + 1],
                 )
 
-        def gate_values(b, h, tiles):
+        def gate_values(b, h, slots):
             if (b, h) not in zt:
-                zt[b, h] = kept("zt_%d%d" % (b, h), [P, N * PACK], BF16)
-            for j in tiles:
+                zt[b, h] = kept("zt_%d%d" % (b, h), [P, PACK, N], BF16)
+            for t in slots:
                 values = bank()
-                for t in range(PACK):
-                    mx_product(values[:, t * P : (t + 1) * P], wvq[h], slice(t * P, (t + 1) * P), xq[b], slice(j * P, (j + 1) * P))
-                nc.vector.scalar_tensor_tensor(
-                    out=zt[b, h][:, j * BANK : (j + 1) * BANK].rearrange("p (n t) -> p n t", t=PACK),
-                    in0=values[:].rearrange("p (t n) -> p n t", t=PACK),
-                    scalar=0.0,
-                    in1=cv[b][:, h * PACK : (h + 1) * PACK].unsqueeze(1).to_broadcast([P, P, PACK]),
+                mx_product(values[:], wvq[h], slice(t * P, (t + 1) * P), xq[b], every)
+                col = h * PACK + t
+                nc.vector.tensor_scalar(
+                    out=zt[b, h][:, t, :], in0=values[:], scalar1=0.0, scalar2=cv[b][:, col : col + 1],
                     op0=ALU.max, op1=ALU.mult,
                 )
 
-        def project(b, h, tiles):
-            cols = slice(h * BANK, (h + 1) * BANK)
+        def project(b, tiles, halves):
+            cols = slice(halves[0] * BANK, (halves[-1] + 1) * BANK)
             for j in tiles:
-                acc = bank()
-                mx_product(acc[:], zq[b], slice(j * P, (j + 1) * P), woq[h], every)
-                result = ring.tile([P, BANK], F32, name="result", tag="result", bufs=8)
-                nc.vector.tensor_tensor(out=result[:], in0=acc[:], in1=bias[:, cols], op=ALU.add)
-                nc.sync.dma_start(out=out[b].rearrange("(p j) f -> p j f", j=TILES)[:, j, cols], in_=result[:])
+                result = ring.tile([P, F], F32, name="result", tag="result", bufs=6)
+                for h in halves:
+                    half = slice(h * BANK, (h + 1) * BANK)
+                    acc = bank()
+                    mx_product(acc[:], zq[b], slice(j * P, (j + 1) * P), woq[h], every)
+                    nc.vector.tensor_tensor(out=result[:, half], in0=acc[:], in1=bias[:, half], op=ALU.add)
+                nc.sync.dma_start(out=out[b].rearrange("(p j) f -> p j f", j=TILES)[:, j, cols], in_=result[:, cols])
 
         on_vector, on_scalar = nc.vector.tensor_copy, nc.scalar.copy
         all4 = range(4)
 
         turn_x(0, 0)
-        g00 = group_channels(on_vector, wk_rows[0, 0])
+        k00 = group_channels(on_vector, wk_rows[0, 0], grouped_tile())
         quantize_x(0, 0)
-        quantize(wkq[0][0], every, g00)
+        quantize(wkq[0][0], every, k00)
         turn_x(0, 1)
-        g10 = group_channels(on_vector, wk_rows[1, 0])
+        k10 = group_channels(on_vector, wk_rows[1, 0], grouped_tile())
         quantize_x(0, 1)
-        quantize(wkq[0][1], every, g10)
+        quantize(wkq[0][1], every, k10)
         score(0)
-        g01 = group_channels(on_scalar, wk_rows[0, 1])
+        k01 = group_channels(on_scalar, wk_rows[0, 1], grouped_tile())
+        k11 = group_channels(on_vector, wk_rows[1, 1], paced_tile())
         score_max(0)
         score_exp(0)
-        g11 = group_channels(on_vector, wk_rows[1, 1])
+        quantize(wkq[1][0], every, k01)
+        quantize(wkq[1][1], every, k11)
         invert_total(0)
-        quantize(wkq[1][0], every, g01)
-        quantize(wkq[1][1], every, g11)
+        o00 = interleave_on_gpsimd(widen_wo(0, 0))
         pool_keys(0, 0, all4)
         turn_x(1, 0)
         turn_x(1, 1)
+        pool_keys(0, 1, all4)
         quantize_x(1, 0)
         quantize_x(1, 1)
         score(1)
+        v00 = group_channels(on_scalar, wv_rows[0, 0], grouped_tile())
         score_max(1)
-        g00 = group_channels(on_scalar, wv_rows[0, 0])
         score_exp(1)
-        pool_keys(0, 1, all4)
+        quantize(wvq[0][0], every, v00)
         invert_total(1)
-        quantize(wvq[0][0], every, g00)
-        g10 = group_channels(on_scalar, wv_rows[1, 0])
+        quantize(woq[0][0], every, o00)
+        v11 = group_channels_on_gpsimd(wv_rows[1, 1])
+        v10 = group_channels(on_scalar, wv_rows[1, 0], grouped_tile())
+        v01 = group_channels(on_scalar, wv_rows[0, 1], grouped_tile())
         pool_keys(1, 0, all4)
-        quantize(wvq[0][1], every, g10)
-        g01 = group_channels(on_scalar, wv_rows[0, 1])
-        pool_keys(1, 1, range(0, 2))
-        quantize(wvq[1][0], every, g01)
-        g11 = group_channels(on_scalar, wv_rows[1, 1])
-        pool_keys(1, 1, range(2, 4))
-        gate_values(0, 0, range(0, 2))
-        quantize(wvq[1][1], every, g11)
-        gate_values(0, 0, range(2, 4))
-        gate_values(0, 1, range(0, 1))
-        quantize(zq[0][0], every, zt[0, 0])
-        gate_values(0, 1, range(1, 4))
-        g00 = group_wo(0, 0)
-        g10 = group_wo(1, 0)
-        gate_values(1, 0, range(0, 1))
-        quantize(zq[0][1], every, zt[0, 1])
-        quantize(woq[0][0], every, g00)
-        gate_values(1, 0, range(1, 4))
-        quantize(woq[0][1], every, g10)
+        pool_keys(1, 1, all4)
+        quantize(wvq[0][1], every, v10)
+        quantize(wvq[1][0], every, v01)
+        quantize(wvq[1][1], every, v11)
+        o10 = interleave_on_gpsimd(widen_wo(1, 0))
+        o01_planes = widen_wo(0, 1)
+        o11_planes = widen_wo(1, 1)
+        gate_values(0, 0, all4)
+        gate_values(0, 1, range(0, 2))
+        quantize(woq[0][1], every, o10)
+        z00 = interleave_on_gpsimd(zt[0, 0])
+        gate_values(0, 1, range(2, 4))
+        z01 = interleave_on_scalar(zt[0, 1])
+        gate_values(1, 0, all4)
         gate_values(1, 1, range(0, 1))
-        quantize(zq[1][0], every, zt[1, 0])
-        project(0, 0, range(0, 2))
+        quantize(zq[0][1], every, z01)
+        quantize(zq[0][0], every, z00)
+        o01 = interleave_on_gpsimd(o01_planes)
+        o11 = interleave_on_scalar(o11_planes)
         gate_values(1, 1, range(1, 4))
-        project(0, 0, range(2, 3))
-        quantize(zq[1][1], every, zt[1, 1])
-        project(0, 0, range(3, 4))
-        g01 = group_wo(0, 1)
-        g11 = group_wo(1, 1)
-        quantize(woq[1][0], every, g01)
-        project(1, 0, range(0, 3))
-        quantize(woq[1][1], every, g11)
-        project(1, 0, range(3, 4))
-        project(0, 1, all4)
-        project(1, 1, all4)
+        z10 = interleave_on_scalar(zt[1, 0])
+        z11 = interleave_on_scalar(zt[1, 1])
+        project(0, range(0, 3), [0])
+        quantize(woq[1][1], every, o11)
+        quantize(woq[1][0], every, o01)
+        project(0, range(3, 4), [0])
+        quantize(zq[1][0], every, z10)
+        project(0, range(0, 3), [1])
+        quantize(zq[1][1], every, z11)
+        project(0, range(3, 4), [1])
+        project(1, range(0, 3), [0, 1])
+        project(1, range(3, 4), [0])
+        project(1, range(3, 4), [1])

@@ -33,7 +33,7 @@ def tile_mobilevitv2separablecontextgate_kernel(tc, x, wi, wk, wv, wo_bytes, wo_
         ctx.enter_context(tc.manual_schedule())
 
         def kept(name, shape, dtype):
-            return keep.tile(shape, dtype, name=name, align_bytes=64)
+            return keep.tile(shape, dtype, name=name, align_bytes=256)
 
         def bank():
             return psum.tile([P, BANK], F32, name="bank", tag="bank")
@@ -77,21 +77,22 @@ def tile_mobilevitv2separablecontextgate_kernel(tc, x, wi, wk, wv, wo_bytes, wo_
 
         x_rows, wk_rows, wv_rows, wo_codes_in = {}, {}, {}, {}
         x_rows[0, 0] = load_x(0, 0)
+        wi_sb = kept("wi_sb", [P, PASSES, PACK], BF16)
+        nc.scalar.dma_start(out=wi_sb[:], in_=wi.rearrange("(g p t) -> p g t", p=P, t=PACK))
         wk_rows[0, 0] = load_weight("wk", wk, 0, 0)
         x_rows[0, 1] = load_x(0, 1)
-        wi_sb = kept("wi_sb", [P, PASSES, PACK], BF16)
-        nc.sync.dma_start(out=wi_sb[:], in_=wi.rearrange("(g p t) -> p g t", p=P, t=PACK))
         wk_rows[1, 0] = load_weight("wk", wk, 1, 0)
         wk_rows[0, 1] = load_weight("wk", wk, 0, 1)
         wk_rows[1, 1] = load_weight("wk", wk, 1, 1)
+        x_rows[1, 0] = load_x(1, 0)
+        x_rows[1, 1] = load_x(1, 1)
+        wv_rows[0, 0] = load_weight("wv", wv, 0, 0)
+        wv_rows[1, 0] = load_weight("wv", wv, 1, 0)
         wo_scale_sb = kept("wo_scale_sb", [P, PASSES, PACK], F32)
         nc.sync.dma_start(out=wo_scale_sb[:], in_=wo_scale.rearrange("(g p t) o -> p g (t o)", p=P, t=PACK))
         wo_codes_in[0] = load_wo(0)
-        x_rows[1, 0] = load_x(1, 0)
-        x_rows[1, 1] = load_x(1, 1)
-        for h in range(2):
-            for g in range(PASSES):
-                wv_rows[g, h] = load_weight("wv", wv, g, h)
+        wv_rows[1, 1] = load_weight("wv", wv, 1, 1)
+        wv_rows[0, 1] = load_weight("wv", wv, 0, 1)
         wo_codes_in[1] = load_wo(1)
         bias = kept("bias", [P, F], BF16)
         nc.sync.dma_start(out=bias[:], in_=bo.partition_broadcast(P))
@@ -105,9 +106,10 @@ def tile_mobilevitv2separablecontextgate_kernel(tc, x, wi, wk, wv, wo_bytes, wo_
         wvq = {h: [mx_operand("wvq_%d%d" % (g, h)) for g in range(PASSES)] for h in range(2)}
         woq = {h: [mx_operand("woq_%d%d" % (g, h)) for g in range(PASSES)] for h in range(2)}
         every = slice(0, BANK)
-        xt, scores, neg_max, expo, total, inv_total, cv, zt = {}, {}, {}, {}, {}, {}, {}, {}
+        result = {(b, j): kept("result_%d%d" % (b, j), [P, F], F32) for b in range(B) for j in range(TILES)}
+        xt, pairs, scores, neg_max, expo, total, inv_total, cv, zt = {}, {}, {}, {}, {}, {}, {}, {}, {}
 
-        def turn_x(b, half):
+        def turn_x(b, half, keep_pairs):
             words = x_rows[b, half][:].bitcast(F32)
             for g in range(PASSES):
                 turned = bank()
@@ -116,27 +118,35 @@ def tile_mobilevitv2separablecontextgate_kernel(tc, x, wi, wk, wv, wo_bytes, wo_
                     first = j * (D // 2) + g * (K_PASS // 2)
                     for u in range(2):
                         nc.tensor.transpose(view[:, j, u, :], words[:, first + u : first + K_PASS // 2 : 2], ident[:])
-                xt[b, g, half] = kept("xt_%d%d%d" % (b, g, half), [P, PAIR * PACK], BF16)
-                dst = xt[b, g, half][:].bitcast(F32).rearrange("p (j r u) -> p j r u", j=2, u=2)
-                nc.scalar.copy(out=dst, in_=view.rearrange("p j u r -> p j r u"))
+                if half == 0:
+                    xt[b, g] = kept("xt_%d%d" % (b, g), [P, N * PACK], BF16)
+                if keep_pairs:
+                    pairs[b, g, half] = kept("pairs_%d%d%d" % (b, g, half), [P, BANK], F32)
+                    nc.scalar.copy(out=pairs[b, g, half][:], in_=turned[:])
+                dst = xt[b, g][:].bitcast(F32)[:, half * BANK : (half + 1) * BANK]
+                nc.scalar.copy(out=dst.rearrange("p (j r u) -> p j r u", j=2, u=2), in_=view.rearrange("p j u r -> p j r u"))
 
-        def quantize_x(b, half):
-            for g in range(PASSES):
-                quantize(xq[b][g], slice(half * PAIR, (half + 1) * PAIR), xt[b, g, half])
+        def quantize_x(b, g, tokens):
+            codes, scales = xq[b][g]
+            values = xt[b, g][:, tokens.start * PACK : tokens.stop * PACK]
+            nc.vector.quantize_mx(out=codes[:, tokens].bitcast(FP8X4), scales=scales[:, tokens], in_=values)
 
-        def score(b):
-            scores[b] = bank()
-            for half in range(2):
-                for g in range(PASSES):
-                    planes = xt[b, g, half][:].rearrange("p (n t) -> p n t", t=PACK)
-                    for t in range(PACK):
-                        nc.tensor.matmul(
-                            scores[b][:, half * PAIR : (half + 1) * PAIR],
-                            lhsT=wi_sb[:, g, t : t + 1].to_broadcast([P, P]),
-                            rhs=planes[:, :, t],
-                            start=(g == 0 and t == 0),
-                            stop=(g == PASSES - 1 and t == PACK - 1),
-                        )
+        def score(b, half, g):
+            if b not in scores:
+                scores[b] = bank()
+            for t in range(PACK):
+                if (b, g, half) in pairs:
+                    words = pairs[b, g, half][:].bitcast(BF16).rearrange("p (j u r e) -> p u e j r", j=2, u=2, e=2)
+                    plane = words[:, t // 2, t % 2]
+                else:
+                    plane = xt[b, g][:, half * PAIR * PACK : (half + 1) * PAIR * PACK].rearrange("p (n t) -> p t n", t=PACK)[:, t]
+                nc.tensor.matmul(
+                    scores[b][:, half * PAIR : (half + 1) * PAIR],
+                    lhsT=wi_sb[:, g, t : t + 1].to_broadcast([P, P]),
+                    rhs=plane,
+                    start=(g == 0 and t == 0),
+                    stop=(g == PASSES - 1 and t == PACK - 1),
+                )
 
         def score_max(b):
             neg_max[b] = kept("neg_max_%d" % b, [P, 1], F32)
@@ -207,52 +217,101 @@ def tile_mobilevitv2separablecontextgate_kernel(tc, x, wi, wk, wv, wo_bytes, wo_
             )
             return grouped
 
+        def in_pairs(items, multiply, empty):
+            for first in range(0, len(items), 2):
+                pair = items[first : first + 2]
+                banks = [multiply(item) for item in pair]
+                for item, acc in reversed(list(zip(pair, banks))):
+                    empty(item, acc)
+
         def pool_keys(b, h, slots):
-            for t in slots:
+            def multiply(t):
                 keys = bank()
                 mx_product(keys[:], wkq[h], slice(t * P, (t + 1) * P), xq[b], every)
-                weighted = ring.tile([P, N], F32, name="weighted", tag="weighted", bufs=2)
+                return keys
+
+            def empty(t, keys):
                 col = h * PACK + t
                 nc.vector.scalar_tensor_tensor(
-                    out=weighted[:], in0=keys[:], scalar=inv_total[b][:], in1=expo[b][:],
+                    out=result[b, t][:, h * BANK : (h + 1) * BANK], in0=keys[:], scalar=inv_total[b][:], in1=expo[b][:],
                     op0=ALU.mult, op1=ALU.mult, accum_out=cv[b][:, col : col + 1],
                 )
 
-        def gate_values(b, h, slots):
+            in_pairs(slots, multiply, empty)
+
+        def gate_values(b, h, tiles):
             if (b, h) not in zt:
-                zt[b, h] = kept("zt_%d%d" % (b, h), [P, PACK, N], BF16)
-            for t in slots:
+                zt[b, h] = kept("zt_%d%d" % (b, h), [P, N * PACK], BF16)
+
+            def multiply(j):
                 values = bank()
-                mx_product(values[:], wvq[h], slice(t * P, (t + 1) * P), xq[b], every)
-                col = h * PACK + t
-                nc.vector.tensor_scalar(
-                    out=zt[b, h][:, t, :], in0=values[:], scalar1=0.0, scalar2=cv[b][:, col : col + 1],
+                for t in range(PACK):
+                    cols = slice(t * P, (t + 1) * P)
+                    mx_product(values[:, cols], wvq[h], cols, xq[b], slice(j * P, (j + 1) * P))
+                return values
+
+            def empty(j, values):
+                nc.vector.scalar_tensor_tensor(
+                    out=zt[b, h][:, j * BANK : (j + 1) * BANK].rearrange("p (n t) -> p n t", t=PACK),
+                    in0=values[:].rearrange("p (t n) -> p n t", t=PACK),
+                    scalar=0.0,
+                    in1=cv[b][:, h * PACK : (h + 1) * PACK].unsqueeze(1).to_broadcast([P, P, PACK]),
                     op0=ALU.max, op1=ALU.mult,
                 )
 
-        def project(b, tiles, halves):
-            cols = slice(halves[0] * BANK, (halves[-1] + 1) * BANK)
-            for j in tiles:
-                result = ring.tile([P, F], F32, name="result", tag="result", bufs=6)
-                for h in halves:
-                    half = slice(h * BANK, (h + 1) * BANK)
-                    acc = bank()
-                    mx_product(acc[:], zq[b], slice(j * P, (j + 1) * P), woq[h], every)
-                    nc.vector.tensor_tensor(out=result[:, half], in0=acc[:], in1=bias[:, half], op=ALU.add)
-                nc.sync.dma_start(out=out[b].rearrange("(p j) f -> p j f", j=TILES)[:, j, cols], in_=result[:, cols])
+            in_pairs(tiles, multiply, empty)
+
+        def project(b, pieces):
+            def multiply(piece):
+                j, h = piece
+                acc = bank()
+                mx_product(acc[:], zq[b], slice(j * P, (j + 1) * P), woq[h], every)
+                return acc
+
+            def empty(piece, acc):
+                j, h = piece
+                half = slice(h * BANK, (h + 1) * BANK)
+                nc.vector.tensor_tensor(out=result[b, j][:, half], in0=acc[:], in1=bias[:, half], op=ALU.add)
+
+            in_pairs(pieces, multiply, empty)
+
+        def store(b, j, cols):
+            nc.sync.dma_start(out=out[b].rearrange("(p j) f -> p j f", j=TILES)[:, j, cols], in_=result[b, j][:, cols])
+
+        def project_aside(b, j, h):
+            half = slice(h * BANK, (h + 1) * BANK)
+            acc = bank()
+            mx_product(acc[:], zq[b], slice(j * P, (j + 1) * P), woq[h], every)
+            nc.scalar.copy(out=result[b, j][:, half], in_=acc[:])
+            nc.gpsimd.tensor_tensor(out=result[b, j][:, half], in0=result[b, j][:, half], in1=bias[:, half], op=ALU.add)
+
+        def project_half(b, h, tiles):
+            project(b, [(j, h) for j in tiles])
+            for j in reversed(tiles):
+                store(b, j, slice(h * BANK, (h + 1) * BANK))
+
+        def project_rows(b, j):
+            project(b, [(j, 0), (j, 1)])
+            store(b, j, slice(0, F))
 
         on_vector, on_scalar = nc.vector.tensor_copy, nc.scalar.copy
         all4 = range(4)
 
-        turn_x(0, 0)
+        first_pair, second_pair = slice(0, PAIR), slice(PAIR, N)
+        turn_x(0, 0, False)
+        score(0, 0, 0)
         k00 = group_channels(on_vector, wk_rows[0, 0], grouped_tile())
-        quantize_x(0, 0)
+        quantize_x(0, 0, first_pair)
         quantize(wkq[0][0], every, k00)
-        turn_x(0, 1)
+        quantize_x(0, 1, first_pair)
+        turn_x(0, 1, False)
+        score(0, 0, 1)
+        score(0, 1, 0)
+        score(0, 1, 1)
         k10 = group_channels(on_vector, wk_rows[1, 0], grouped_tile())
-        quantize_x(0, 1)
+        quantize_x(0, 0, second_pair)
         quantize(wkq[0][1], every, k10)
-        score(0)
+        quantize_x(0, 1, second_pair)
         k01 = group_channels(on_scalar, wk_rows[0, 1], grouped_tile())
         k11 = group_channels(on_vector, wk_rows[1, 1], paced_tile())
         score_max(0)
@@ -260,54 +319,58 @@ def tile_mobilevitv2separablecontextgate_kernel(tc, x, wi, wk, wv, wo_bytes, wo_
         quantize(wkq[1][0], every, k01)
         quantize(wkq[1][1], every, k11)
         invert_total(0)
-        o00 = interleave_on_gpsimd(widen_wo(0, 0))
+        v00 = group_channels_on_gpsimd(wv_rows[0, 0])
         pool_keys(0, 0, all4)
-        turn_x(1, 0)
-        turn_x(1, 1)
+        turn_x(1, 0, True)
+        turn_x(1, 1, True)
         pool_keys(0, 1, all4)
-        quantize_x(1, 0)
-        quantize_x(1, 1)
-        score(1)
-        v00 = group_channels(on_scalar, wv_rows[0, 0], grouped_tile())
+        quantize_x(1, 0, every)
+        quantize_x(1, 1, every)
+        for half in range(2):
+            for g in range(PASSES):
+                score(1, half, g)
+        v10 = group_channels(on_scalar, wv_rows[1, 0], grouped_tile())
         score_max(1)
         score_exp(1)
+        quantize(wvq[0][1], every, v10)
         quantize(wvq[0][0], every, v00)
         invert_total(1)
-        quantize(woq[0][0], every, o00)
         v11 = group_channels_on_gpsimd(wv_rows[1, 1])
-        v10 = group_channels(on_scalar, wv_rows[1, 0], grouped_tile())
+        o00_planes = widen_wo(0, 0)
         v01 = group_channels(on_scalar, wv_rows[0, 1], grouped_tile())
         pool_keys(1, 0, all4)
-        pool_keys(1, 1, all4)
-        quantize(wvq[0][1], every, v10)
+        pool_keys(1, 1, range(0, 2))
         quantize(wvq[1][0], every, v01)
         quantize(wvq[1][1], every, v11)
-        o10 = interleave_on_gpsimd(widen_wo(1, 0))
+        o00 = interleave_on_gpsimd(o00_planes)
+        o10_planes = widen_wo(1, 0)
         o01_planes = widen_wo(0, 1)
-        o11_planes = widen_wo(1, 1)
+        pool_keys(1, 1, range(2, 4))
         gate_values(0, 0, all4)
-        gate_values(0, 1, range(0, 2))
+        quantize(woq[0][0], every, o00)
+        o10 = interleave_on_gpsimd(o10_planes)
+        o01 = interleave_on_scalar(o01_planes)
+        o11 = interleave_on_scalar(widen_wo(1, 1))
+        gate_values(0, 1, all4)
+        gate_values(1, 0, range(0, 2))
+        quantize(zq[0][0], every, zt[0, 0])
+        quantize(zq[0][1], every, zt[0, 1])
         quantize(woq[0][1], every, o10)
-        z00 = interleave_on_gpsimd(zt[0, 0])
-        gate_values(0, 1, range(2, 4))
-        z01 = interleave_on_scalar(zt[0, 1])
-        gate_values(1, 0, all4)
-        gate_values(1, 1, range(0, 1))
-        quantize(zq[0][1], every, z01)
-        quantize(zq[0][0], every, z00)
-        o01 = interleave_on_gpsimd(o01_planes)
-        o11 = interleave_on_scalar(o11_planes)
-        gate_values(1, 1, range(1, 4))
-        z10 = interleave_on_scalar(zt[1, 0])
-        z11 = interleave_on_scalar(zt[1, 1])
-        project(0, range(0, 3), [0])
-        quantize(woq[1][1], every, o11)
+        gate_values(1, 0, range(2, 4))
+        gate_values(1, 1, range(0, 2))
+        project_aside(0, 2, 0)
+        project_aside(0, 3, 0)
+        project_half(0, 0, range(0, 2))
+        gate_values(1, 1, range(2, 4))
+        store(0, 2, slice(0, BANK))
+        store(0, 3, slice(0, BANK))
         quantize(woq[1][0], every, o01)
-        project(0, range(3, 4), [0])
-        quantize(zq[1][0], every, z10)
-        project(0, range(0, 3), [1])
-        quantize(zq[1][1], every, z11)
-        project(0, range(3, 4), [1])
-        project(1, range(0, 3), [0, 1])
-        project(1, range(3, 4), [0])
-        project(1, range(3, 4), [1])
+        quantize(woq[1][1], every, o11)
+        quantize(zq[1][0], every, zt[1, 0])
+        quantize(zq[1][1], every, zt[1, 1])
+        project_half(0, 1, range(0, 2))
+        project_half(0, 1, range(2, 4))
+        for j in range(TILES - 1):
+            project_rows(1, j)
+        project_half(1, 0, range(3, 4))
+        project_half(1, 1, range(3, 4))

@@ -18,7 +18,7 @@ ACT = mybir.ActivationFunctionType
 P = 128
 PACK = 4
 K_PASS = P * PACK
-PASSES = 2
+PASSES = D // K_PASS
 BANK = 512
 TILES = N // P
 PAIR = 2 * P
@@ -41,9 +41,9 @@ def tile_mobilevitv2separablecontextgate_kernel(tc, x, wi, wk, wv, wo_bytes, wo_
         def mx_operand(name):
             return kept(name + "_codes", [P, BANK], U32), kept(name + "_scales", [P, BANK], U8)
 
-        def quantize(operand, cols, grouped):
+        def quantize(operand, grouped):
             codes, scales = operand
-            nc.vector.quantize_mx(out=codes[:, cols].bitcast(FP8X4), scales=scales[:, cols], in_=grouped[:])
+            nc.vector.quantize_mx(out=codes[:].bitcast(FP8X4), scales=scales[:], in_=grouped[:])
 
         def mx_product(acc, stationary, s_cols, moving, m_cols):
             for g in range(PASSES):
@@ -57,9 +57,9 @@ def tile_mobilevitv2separablecontextgate_kernel(tc, x, wi, wk, wv, wo_bytes, wo_
                     stop=(g == PASSES - 1),
                 )
 
-        def load_x(b, half):
-            rows = kept("x_rows_%d%d" % (b, half), [P, 2 * D], BF16)
-            src = x[b].rearrange("(p j) d -> p j d", j=TILES)[:, 2 * half : 2 * half + 2, :]
+        def load_x(b, pair):
+            rows = kept("x_rows_%d%d" % (b, pair), [P, 2 * D], BF16)
+            src = x[b].rearrange("(p j) d -> p j d", j=TILES)[:, 2 * pair : 2 * pair + 2, :]
             nc.sync.dma_start(out=rows[:].rearrange("p (j d) -> p j d", j=2), in_=src)
             return rows
 
@@ -70,30 +70,29 @@ def tile_mobilevitv2separablecontextgate_kernel(tc, x, wi, wk, wv, wo_bytes, wo_
             return rows
 
         def load_wo(g):
-            codes = kept("wo_bytes_sb_%d" % g, [P, PACK * F], U8)
+            raw = kept("wo_bytes_sb_%d" % g, [P, PACK * F], U8)
             src = wo_bytes[g * K_PASS : (g + 1) * K_PASS, :].rearrange("(p t) f -> p (t f)", t=PACK)
-            nc.sync.dma_start(out=codes[:], in_=src)
-            return codes
+            nc.sync.dma_start(out=raw[:], in_=src)
+            return raw
 
-        x_rows, wk_rows, wv_rows, wo_codes_in = {}, {}, {}, {}
+        x_rows, wk_rows, wv_rows, wo_raw = {}, {}, {}, {}
         x_rows[0, 0] = load_x(0, 0)
         wi_sb = kept("wi_sb", [P, PASSES, PACK], BF16)
         nc.scalar.dma_start(out=wi_sb[:], in_=wi.rearrange("(g p t) -> p g t", p=P, t=PACK))
+        wo_scale_sb = kept("wo_scale_sb", [P, PASSES, PACK], F32)
+        nc.scalar.dma_start(out=wo_scale_sb[:], in_=wo_scale.rearrange("(g p t) o -> p g (t o)", p=P, t=PACK))
         wk_rows[0, 0] = load_weight("wk", wk, 0, 0)
         x_rows[0, 1] = load_x(0, 1)
         wk_rows[1, 0] = load_weight("wk", wk, 1, 0)
         wk_rows[0, 1] = load_weight("wk", wk, 0, 1)
         wk_rows[1, 1] = load_weight("wk", wk, 1, 1)
+        wo_raw[0] = load_wo(0)
         x_rows[1, 0] = load_x(1, 0)
         x_rows[1, 1] = load_x(1, 1)
-        wv_rows[0, 0] = load_weight("wv", wv, 0, 0)
-        wv_rows[1, 0] = load_weight("wv", wv, 1, 0)
-        wo_scale_sb = kept("wo_scale_sb", [P, PASSES, PACK], F32)
-        nc.sync.dma_start(out=wo_scale_sb[:], in_=wo_scale.rearrange("(g p t) o -> p g (t o)", p=P, t=PACK))
-        wo_codes_in[0] = load_wo(0)
-        wv_rows[1, 1] = load_weight("wv", wv, 1, 1)
-        wv_rows[0, 1] = load_weight("wv", wv, 0, 1)
-        wo_codes_in[1] = load_wo(1)
+        for h in range(2):
+            for g in range(PASSES):
+                wv_rows[g, h] = load_weight("wv", wv, g, h)
+        wo_raw[1] = load_wo(1)
         bias = kept("bias", [P, F], BF16)
         nc.sync.dma_start(out=bias[:], in_=bo.partition_broadcast(P))
 
@@ -107,10 +106,10 @@ def tile_mobilevitv2separablecontextgate_kernel(tc, x, wi, wk, wv, wo_bytes, wo_
         woq = {h: [mx_operand("woq_%d%d" % (g, h)) for g in range(PASSES)] for h in range(2)}
         every = slice(0, BANK)
         result = {(b, j): kept("result_%d%d" % (b, j), [P, F], F32) for b in range(B) for j in range(TILES)}
-        xt, pairs, scores, neg_max, expo, total, inv_total, cv, zt = {}, {}, {}, {}, {}, {}, {}, {}, {}
+        xt, words_kept, scores, neg_max, expo, total, inv_total, cv, zt = {}, {}, {}, {}, {}, {}, {}, {}, {}
 
-        def turn_x(b, half, keep_pairs):
-            words = x_rows[b, half][:].bitcast(F32)
+        def turn_x(b, pair, keep_words):
+            words = x_rows[b, pair][:].bitcast(F32)
             for g in range(PASSES):
                 turned = bank()
                 view = turned[:].rearrange("p (j u r) -> p j u r", j=2, u=2)
@@ -118,30 +117,33 @@ def tile_mobilevitv2separablecontextgate_kernel(tc, x, wi, wk, wv, wo_bytes, wo_
                     first = j * (D // 2) + g * (K_PASS // 2)
                     for u in range(2):
                         nc.tensor.transpose(view[:, j, u, :], words[:, first + u : first + K_PASS // 2 : 2], ident[:])
-                if half == 0:
+                if pair == 0:
                     xt[b, g] = kept("xt_%d%d" % (b, g), [P, N * PACK], BF16)
-                if keep_pairs:
-                    pairs[b, g, half] = kept("pairs_%d%d%d" % (b, g, half), [P, BANK], F32)
-                    nc.scalar.copy(out=pairs[b, g, half][:], in_=turned[:])
-                dst = xt[b, g][:].bitcast(F32)[:, half * BANK : (half + 1) * BANK]
-                nc.scalar.copy(out=dst.rearrange("p (j r u) -> p j r u", j=2, u=2), in_=view.rearrange("p j u r -> p j r u"))
+                if keep_words:
+                    words_kept[b, g, pair] = kept("words_%d%d%d" % (b, g, pair), [P, BANK], F32)
+                    nc.scalar.copy(out=words_kept[b, g, pair][:], in_=turned[:])
+                dst = xt[b, g][:].bitcast(F32)[:, pair * BANK : (pair + 1) * BANK]
+                nc.scalar.copy(
+                    out=dst.rearrange("p (j r u) -> p j r u", j=2, u=2), in_=view.rearrange("p j u r -> p j r u")
+                )
 
         def quantize_x(b, g, tokens):
             codes, scales = xq[b][g]
             values = xt[b, g][:, tokens.start * PACK : tokens.stop * PACK]
             nc.vector.quantize_mx(out=codes[:, tokens].bitcast(FP8X4), scales=scales[:, tokens], in_=values)
 
-        def score(b, half, g):
+        def score(b, pair, g):
             if b not in scores:
                 scores[b] = bank()
             for t in range(PACK):
-                if (b, g, half) in pairs:
-                    words = pairs[b, g, half][:].bitcast(BF16).rearrange("p (j u r e) -> p u e j r", j=2, u=2, e=2)
-                    plane = words[:, t // 2, t % 2]
+                if (b, g, pair) in words_kept:
+                    halves = words_kept[b, g, pair][:].bitcast(BF16)
+                    plane = halves.rearrange("p (j u r e) -> p u e j r", j=2, u=2, e=2)[:, t // 2, t % 2]
                 else:
-                    plane = xt[b, g][:, half * PAIR * PACK : (half + 1) * PAIR * PACK].rearrange("p (n t) -> p t n", t=PACK)[:, t]
+                    grouped = xt[b, g][:, pair * PAIR * PACK : (pair + 1) * PAIR * PACK]
+                    plane = grouped.rearrange("p (n t) -> p t n", t=PACK)[:, t]
                 nc.tensor.matmul(
-                    scores[b][:, half * PAIR : (half + 1) * PAIR],
+                    scores[b][:, pair * PAIR : (pair + 1) * PAIR],
                     lhsT=wi_sb[:, g, t : t + 1].to_broadcast([P, P]),
                     rhs=plane,
                     start=(g == 0 and t == 0),
@@ -163,11 +165,10 @@ def tile_mobilevitv2separablecontextgate_kernel(tc, x, wi, wk, wv, wo_bytes, wo_
 
         def invert_total(b):
             inv_total[b] = kept("inv_total_%d" % b, [P, 1], F32)
-            cv[b] = kept("cv_%d" % b, [P, 2 * PACK], F32)
             nc.vector.reciprocal(out=inv_total[b][:], in_=total[b][:])
 
         def grouped_tile():
-            return ring.tile([P, BANK * PACK], BF16, name="grouped", tag="grouped", bufs=4, align_bytes=64)
+            return ring.tile([P, BANK * PACK], BF16, name="grouped", tag="grouped", bufs=3, align_bytes=64)
 
         def paced_tile():
             return ring.tile([P, BANK * PACK], BF16, name="paced", tag="paced", bufs=1, align_bytes=64)
@@ -179,28 +180,32 @@ def tile_mobilevitv2separablecontextgate_kernel(tc, x, wi, wk, wv, wo_bytes, wo_
             )
             return grouped
 
+        def move_on_gpsimd(dst, src):
+            nc.gpsimd.tensor_scalar(out=dst, in0=src, scalar1=1.0, scalar2=0.0, op0=ALU.mult, op1=ALU.add)
+
         def group_channels_on_gpsimd(rows):
             grouped = paced_tile()
-            nc.gpsimd.tensor_scalar(
-                out=grouped[:].rearrange("p (t m j) -> p t m j", t=PACK, j=PACK),
-                in0=rows[:].rearrange("p j (m t) -> p t m j", t=PACK),
-                scalar1=1.0, scalar2=0.0, op0=ALU.mult, op1=ALU.add,
+            move_on_gpsimd(
+                grouped[:].rearrange("p (t m j) -> p t m j", t=PACK, j=PACK),
+                rows[:].rearrange("p j (m t) -> p t m j", t=PACK),
             )
             return grouped
 
-        def widen_wo(g, h):
-            planes = ring.tile([P, PACK, BANK], BF16, name="planes", tag="planes", bufs=3, align_bytes=64)
-            for t in range(PACK):
+        def plane_tile():
+            return ring.tile([P, PACK, BANK], BF16, name="planes", tag="planes", bufs=3, align_bytes=64)
+
+        def widen_wo(g, h, planes, slots):
+            for t in slots:
                 first = t * F + h * BANK
                 nc.scalar.activation(
                     out=planes[:, t, :],
-                    in_=wo_codes_in[g][:, first : first + BANK].bitcast(FP8),
+                    in_=wo_raw[g][:, first : first + BANK].bitcast(FP8),
                     func=ACT.Copy,
                     scale=wo_scale_sb[:, g, t : t + 1],
                 )
             return planes
 
-        def interleave_on_scalar(planes):
+        def group_planes_on_scalar(planes):
             grouped = grouped_tile()
             nc.scalar.copy(
                 out=grouped[:].rearrange("p (c i t) -> p c t i", i=4, t=PACK),
@@ -208,23 +213,22 @@ def tile_mobilevitv2separablecontextgate_kernel(tc, x, wi, wk, wv, wo_bytes, wo_
             )
             return grouped
 
-        def interleave_on_gpsimd(planes):
+        def group_planes_on_gpsimd(planes):
             grouped = paced_tile()
-            nc.gpsimd.tensor_scalar(
-                out=grouped[:].rearrange("p (n t) -> p n t", t=PACK),
-                in0=planes[:].rearrange("p t n -> p n t"),
-                scalar1=1.0, scalar2=0.0, op0=ALU.mult, op1=ALU.add,
-            )
+            move_on_gpsimd(grouped[:].rearrange("p (n t) -> p n t", t=PACK), planes[:].rearrange("p t n -> p n t"))
             return grouped
 
-        def in_pairs(items, multiply, empty):
+        def two_banks_at_a_time(items, multiply, empty):
             for first in range(0, len(items), 2):
-                pair = items[first : first + 2]
-                banks = [multiply(item) for item in pair]
-                for item, acc in reversed(list(zip(pair, banks))):
+                both = items[first : first + 2]
+                banks = [multiply(item) for item in both]
+                for item, acc in reversed(list(zip(both, banks))):
                     empty(item, acc)
 
         def pool_keys(b, h, slots):
+            if b not in cv:
+                cv[b] = kept("cv_%d" % b, [P, 2 * PACK], F32)
+
             def multiply(t):
                 keys = bank()
                 mx_product(keys[:], wkq[h], slice(t * P, (t + 1) * P), xq[b], every)
@@ -233,11 +237,16 @@ def tile_mobilevitv2separablecontextgate_kernel(tc, x, wi, wk, wv, wo_bytes, wo_
             def empty(t, keys):
                 col = h * PACK + t
                 nc.vector.scalar_tensor_tensor(
-                    out=result[b, t][:, h * BANK : (h + 1) * BANK], in0=keys[:], scalar=inv_total[b][:], in1=expo[b][:],
-                    op0=ALU.mult, op1=ALU.mult, accum_out=cv[b][:, col : col + 1],
+                    out=result[b, t][:, h * BANK : (h + 1) * BANK],
+                    in0=keys[:],
+                    scalar=inv_total[b][:],
+                    in1=expo[b][:],
+                    op0=ALU.mult,
+                    op1=ALU.mult,
+                    accum_out=cv[b][:, col : col + 1],
                 )
 
-            in_pairs(slots, multiply, empty)
+            two_banks_at_a_time(slots, multiply, empty)
 
         def gate_values(b, h, tiles):
             if (b, h) not in zt:
@@ -256,10 +265,28 @@ def tile_mobilevitv2separablecontextgate_kernel(tc, x, wi, wk, wv, wo_bytes, wo_
                     in0=values[:].rearrange("p (t n) -> p n t", t=PACK),
                     scalar=0.0,
                     in1=cv[b][:, h * PACK : (h + 1) * PACK].unsqueeze(1).to_broadcast([P, P, PACK]),
-                    op0=ALU.max, op1=ALU.mult,
+                    op0=ALU.max,
+                    op1=ALU.mult,
                 )
 
-            in_pairs(tiles, multiply, empty)
+            two_banks_at_a_time(tiles, multiply, empty)
+
+        def gate_values_on_scalar(b, h):
+            planes = plane_tile()
+            rectified = kept("rectified", [P, PACK * N], F32)
+            for t in range(PACK):
+                values = bank()
+                mx_product(values[:], wvq[h], slice(t * P, (t + 1) * P), xq[b], every)
+                nc.scalar.activation(out=rectified[:, t * N : (t + 1) * N], in_=values[:], func=ACT.Relu)
+            for t in range(PACK):
+                col = h * PACK + t
+                nc.scalar.activation(
+                    out=planes[:, t, :],
+                    in_=rectified[:, t * N : (t + 1) * N],
+                    func=ACT.Copy,
+                    scale=cv[b][:, col : col + 1],
+                )
+            return planes
 
         def project(b, pieces):
             def multiply(piece):
@@ -270,20 +297,14 @@ def tile_mobilevitv2separablecontextgate_kernel(tc, x, wi, wk, wv, wo_bytes, wo_
 
             def empty(piece, acc):
                 j, h = piece
-                half = slice(h * BANK, (h + 1) * BANK)
-                nc.vector.tensor_tensor(out=result[b, j][:, half], in0=acc[:], in1=bias[:, half], op=ALU.add)
+                cols = slice(h * BANK, (h + 1) * BANK)
+                nc.vector.tensor_tensor(out=result[b, j][:, cols], in0=acc[:], in1=bias[:, cols], op=ALU.add)
 
-            in_pairs(pieces, multiply, empty)
+            two_banks_at_a_time(pieces, multiply, empty)
 
         def store(b, j, cols):
-            nc.sync.dma_start(out=out[b].rearrange("(p j) f -> p j f", j=TILES)[:, j, cols], in_=result[b, j][:, cols])
-
-        def project_aside(b, j, h):
-            half = slice(h * BANK, (h + 1) * BANK)
-            acc = bank()
-            mx_product(acc[:], zq[b], slice(j * P, (j + 1) * P), woq[h], every)
-            nc.scalar.copy(out=result[b, j][:, half], in_=acc[:])
-            nc.gpsimd.tensor_tensor(out=result[b, j][:, half], in0=result[b, j][:, half], in1=bias[:, half], op=ALU.add)
+            dst = out[b].rearrange("(p j) f -> p j f", j=TILES)[:, j, cols]
+            nc.sync.dma_start(out=dst, in_=result[b, j][:, cols])
 
         def project_half(b, h, tiles):
             project(b, [(j, h) for j in tiles])
@@ -295,14 +316,14 @@ def tile_mobilevitv2separablecontextgate_kernel(tc, x, wi, wk, wv, wo_bytes, wo_
             store(b, j, slice(0, F))
 
         on_vector, on_scalar = nc.vector.tensor_copy, nc.scalar.copy
-        all4 = range(4)
-
+        all_four, first_two, last_two = range(4), range(0, 2), range(2, 4)
         first_pair, second_pair = slice(0, PAIR), slice(PAIR, N)
+
         turn_x(0, 0, False)
         score(0, 0, 0)
         k00 = group_channels(on_vector, wk_rows[0, 0], grouped_tile())
         quantize_x(0, 0, first_pair)
-        quantize(wkq[0][0], every, k00)
+        quantize(wkq[0][0], k00)
         quantize_x(0, 1, first_pair)
         turn_x(0, 1, False)
         score(0, 0, 1)
@@ -310,67 +331,69 @@ def tile_mobilevitv2separablecontextgate_kernel(tc, x, wi, wk, wv, wo_bytes, wo_
         score(0, 1, 1)
         k10 = group_channels(on_vector, wk_rows[1, 0], grouped_tile())
         quantize_x(0, 0, second_pair)
-        quantize(wkq[0][1], every, k10)
+        quantize(wkq[0][1], k10)
         quantize_x(0, 1, second_pair)
         k01 = group_channels(on_scalar, wk_rows[0, 1], grouped_tile())
         k11 = group_channels(on_vector, wk_rows[1, 1], paced_tile())
+        o00_planes = widen_wo(0, 0, plane_tile(), first_two)
         score_max(0)
         score_exp(0)
-        quantize(wkq[1][0], every, k01)
-        quantize(wkq[1][1], every, k11)
+        widen_wo(0, 0, o00_planes, last_two)
+        quantize(wkq[1][0], k01)
+        quantize(wkq[1][1], k11)
         invert_total(0)
+
         v00 = group_channels_on_gpsimd(wv_rows[0, 0])
-        pool_keys(0, 0, all4)
+        pool_keys(0, 0, all_four)
         turn_x(1, 0, True)
         turn_x(1, 1, True)
-        pool_keys(0, 1, all4)
-        quantize_x(1, 0, every)
-        quantize_x(1, 1, every)
-        for half in range(2):
+        pool_keys(0, 1, all_four)
+        for g in range(PASSES):
+            quantize_x(1, g, every)
+        for pair in range(2):
             for g in range(PASSES):
-                score(1, half, g)
+                score(1, pair, g)
         v10 = group_channels(on_scalar, wv_rows[1, 0], grouped_tile())
         score_max(1)
         score_exp(1)
-        quantize(wvq[0][1], every, v10)
-        quantize(wvq[0][0], every, v00)
+        quantize(wvq[0][1], v10)
+        quantize(wvq[0][0], v00)
         invert_total(1)
+
         v11 = group_channels_on_gpsimd(wv_rows[1, 1])
-        o00_planes = widen_wo(0, 0)
         v01 = group_channels(on_scalar, wv_rows[0, 1], grouped_tile())
-        pool_keys(1, 0, all4)
-        pool_keys(1, 1, range(0, 2))
-        quantize(wvq[1][0], every, v01)
-        quantize(wvq[1][1], every, v11)
-        o00 = interleave_on_gpsimd(o00_planes)
-        o10_planes = widen_wo(1, 0)
-        o01_planes = widen_wo(0, 1)
-        pool_keys(1, 1, range(2, 4))
-        gate_values(0, 0, all4)
-        quantize(woq[0][0], every, o00)
-        o10 = interleave_on_gpsimd(o10_planes)
-        o01 = interleave_on_scalar(o01_planes)
-        o11 = interleave_on_scalar(widen_wo(1, 1))
-        gate_values(0, 1, all4)
-        gate_values(1, 0, range(0, 2))
-        quantize(zq[0][0], every, zt[0, 0])
-        quantize(zq[0][1], every, zt[0, 1])
-        quantize(woq[0][1], every, o10)
-        gate_values(1, 0, range(2, 4))
-        gate_values(1, 1, range(0, 2))
-        project_aside(0, 2, 0)
-        project_aside(0, 3, 0)
-        project_half(0, 0, range(0, 2))
-        gate_values(1, 1, range(2, 4))
-        store(0, 2, slice(0, BANK))
-        store(0, 3, slice(0, BANK))
-        quantize(woq[1][0], every, o01)
-        quantize(woq[1][1], every, o11)
-        quantize(zq[1][0], every, zt[1, 0])
-        quantize(zq[1][1], every, zt[1, 1])
-        project_half(0, 1, range(0, 2))
-        project_half(0, 1, range(2, 4))
+        pool_keys(1, 0, all_four)
+        pool_keys(1, 1, first_two)
+        quantize(wvq[1][0], v01)
+        quantize(wvq[1][1], v11)
+
+        o00 = group_planes_on_gpsimd(o00_planes)
+        o10_planes = widen_wo(1, 0, plane_tile(), all_four)
+        o01_planes = widen_wo(0, 1, plane_tile(), all_four)
+        pool_keys(1, 1, last_two)
+        gate_values(0, 0, all_four)
+        quantize(woq[0][0], o00)
+        o10 = group_planes_on_gpsimd(o10_planes)
+        o01 = group_planes_on_scalar(o01_planes)
+        o11_planes = widen_wo(1, 1, plane_tile(), all_four)
+        gate_values(0, 1, all_four)
+        gate_values(1, 0, first_two)
+        z11 = group_planes_on_scalar(gate_values_on_scalar(1, 1))
+        quantize(zq[0][0], zt[0, 0])
+        quantize(zq[0][1], zt[0, 1])
+        quantize(woq[1][0], o01)
+        quantize(woq[0][1], o10)
+
+        o11 = group_planes_on_gpsimd(o11_planes)
+        gate_values(1, 0, last_two)
+        project_half(0, 0, first_two)
+        project_half(0, 0, last_two)
+        quantize(woq[1][1], o11)
+        quantize(zq[1][0], zt[1, 0])
+        quantize(zq[1][1], z11)
+        project_half(0, 1, first_two)
+        project_half(0, 1, last_two)
         for j in range(TILES - 1):
             project_rows(1, j)
-        project_half(1, 0, range(3, 4))
-        project_half(1, 1, range(3, 4))
+        for h in range(2):
+            project_half(1, h, range(TILES - 1, TILES))

from contextlib import ExitStack

import concourse.mybir as mybir
from concourse.masks import make_identity

B, N, D, E, F = 2, 512, 1024, 1024, 1024
FLOPS = 2 * B * N * (D * E * 2 + E * F) + 2 * B * N * D + 2 * B * N * E

F32 = mybir.dt.float32
BF16 = mybir.dt.bfloat16
U32 = mybir.dt.uint32
U8 = mybir.dt.uint8
FP8 = mybir.dt.float8_e4m3fn
FP8X4 = mybir.dt.float8_e4m3fn_x4
ALU = mybir.AluOpType
ACT = mybir.ActivationFunctionType

P = 128
PACK = 4
K_PASS = P * PACK
PASSES = D // K_PASS
BANK = 512
TILES = N // P
PAIR = 2 * P


def tile_mobilevitv2separablecontextgate_kernel(tc, x, wi, wk, wv, wo_bytes, wo_scale, bo, out):
    nc = tc.nc
    with ExitStack() as ctx:
        keep = ctx.enter_context(tc.tile_pool(name="keep", bufs=1))
        ring = ctx.enter_context(tc.tile_pool(name="ring", bufs=1))
        psum = ctx.enter_context(tc.psum_pool(name="psum", bufs=8))
        ctx.enter_context(tc.manual_schedule())

        def kept(name, shape, dtype):
            return keep.tile(shape, dtype, name=name, align_bytes=256)

        def bank():
            return psum.tile([P, BANK], F32, name="bank", tag="bank")

        def mx_operand(name):
            return kept(name + "_codes", [P, BANK], U32), kept(name + "_scales", [P, BANK], U8)

        def quantize(operand, grouped):
            codes, scales = operand
            nc.vector.quantize_mx(out=codes[:].bitcast(FP8X4), scales=scales[:], in_=grouped[:])

        def mx_product(acc, stationary, s_cols, moving, m_cols):
            for g in range(PASSES):
                nc.tensor.matmul_mx(
                    out=acc,
                    lhsT=stationary[g][0][:, s_cols].bitcast(FP8X4),
                    lhsT_scale=stationary[g][1][:, s_cols],
                    rhs=moving[g][0][:, m_cols].bitcast(FP8X4),
                    rhs_scale=moving[g][1][:, m_cols],
                    start=(g == 0),
                    stop=(g == PASSES - 1),
                )

        def load_x(b, pair):
            rows = kept("x_rows_%d%d" % (b, pair), [P, 2 * D], BF16)
            src = x[b].rearrange("(p j) d -> p j d", j=TILES)[:, 2 * pair : 2 * pair + 2, :]
            nc.sync.dma_start(out=rows[:].rearrange("p (j d) -> p j d", j=2), in_=src)
            return rows

        def load_weight(name, w, g, h):
            rows = kept("%s_rows_%d%d" % (name, g, h), [P, PACK, BANK], BF16)
            src = w[g * K_PASS : (g + 1) * K_PASS, h * BANK : (h + 1) * BANK]
            nc.sync.dma_start(out=rows[:], in_=src.rearrange("(p j) e -> p j e", j=PACK))
            return rows

        def load_wo(g):
            raw = kept("wo_bytes_sb_%d" % g, [P, PACK * F], U8)
            src = wo_bytes[g * K_PASS : (g + 1) * K_PASS, :].rearrange("(p t) f -> p (t f)", t=PACK)
            nc.sync.dma_start(out=raw[:], in_=src)
            return raw

        x_rows, wk_rows, wv_rows, wo_raw = {}, {}, {}, {}
        x_rows[0, 0] = load_x(0, 0)
        wi_sb = kept("wi_sb", [P, PASSES, PACK], BF16)
        nc.scalar.dma_start(out=wi_sb[:], in_=wi.rearrange("(g p t) -> p g t", p=P, t=PACK))
        wo_scale_sb = kept("wo_scale_sb", [P, PASSES, PACK], F32)
        nc.scalar.dma_start(out=wo_scale_sb[:], in_=wo_scale.rearrange("(g p t) o -> p g (t o)", p=P, t=PACK))
        wk_rows[0, 0] = load_weight("wk", wk, 0, 0)
        x_rows[0, 1] = load_x(0, 1)
        wk_rows[1, 0] = load_weight("wk", wk, 1, 0)
        wk_rows[0, 1] = load_weight("wk", wk, 0, 1)
        wk_rows[1, 1] = load_weight("wk", wk, 1, 1)
        wo_raw[0] = load_wo(0)
        x_rows[1, 0] = load_x(1, 0)
        x_rows[1, 1] = load_x(1, 1)
        for h in range(2):
            for g in range(PASSES):
                wv_rows[g, h] = load_weight("wv", wv, g, h)
        wo_raw[1] = load_wo(1)
        bias = kept("bias", [P, F], BF16)
        nc.sync.dma_start(out=bias[:], in_=bo.partition_broadcast(P))

        ident = kept("ident", [P, P], F32)
        make_identity(nc, ident[:])

        xq = {b: [mx_operand("xq_%d%d" % (b, g)) for g in range(PASSES)] for b in range(B)}
        zq = {b: [mx_operand("zq_%d%d" % (b, g)) for g in range(PASSES)] for b in range(B)}
        wkq = {h: [mx_operand("wkq_%d%d" % (g, h)) for g in range(PASSES)] for h in range(2)}
        wvq = {h: [mx_operand("wvq_%d%d" % (g, h)) for g in range(PASSES)] for h in range(2)}
        woq = {h: [mx_operand("woq_%d%d" % (g, h)) for g in range(PASSES)] for h in range(2)}
        every = slice(0, BANK)
        result = {(b, j): kept("result_%d%d" % (b, j), [P, F], F32) for b in range(B) for j in range(TILES)}
        xt, words_kept, scores, neg_max, expo, total, inv_total, cv, zt = {}, {}, {}, {}, {}, {}, {}, {}, {}

        def turn_x(b, pair, keep_words):
            words = x_rows[b, pair][:].bitcast(F32)
            for g in range(PASSES):
                turned = bank()
                view = turned[:].rearrange("p (j u r) -> p j u r", j=2, u=2)
                for j in range(2):
                    first = j * (D // 2) + g * (K_PASS // 2)
                    for u in range(2):
                        nc.tensor.transpose(view[:, j, u, :], words[:, first + u : first + K_PASS // 2 : 2], ident[:])
                if pair == 0:
                    xt[b, g] = kept("xt_%d%d" % (b, g), [P, N * PACK], BF16)
                if keep_words:
                    words_kept[b, g, pair] = kept("words_%d%d%d" % (b, g, pair), [P, BANK], F32)
                    nc.scalar.copy(out=words_kept[b, g, pair][:], in_=turned[:])
                dst = xt[b, g][:].bitcast(F32)[:, pair * BANK : (pair + 1) * BANK]
                nc.scalar.copy(
                    out=dst.rearrange("p (j r u) -> p j r u", j=2, u=2), in_=view.rearrange("p j u r -> p j r u")
                )

        def quantize_x(b, g, tokens):
            codes, scales = xq[b][g]
            values = xt[b, g][:, tokens.start * PACK : tokens.stop * PACK]
            nc.vector.quantize_mx(out=codes[:, tokens].bitcast(FP8X4), scales=scales[:, tokens], in_=values)

        def score(b, pair, g):
            if b not in scores:
                scores[b] = bank()
            for t in range(PACK):
                if (b, g, pair) in words_kept:
                    halves = words_kept[b, g, pair][:].bitcast(BF16)
                    plane = halves.rearrange("p (j u r e) -> p u e j r", j=2, u=2, e=2)[:, t // 2, t % 2]
                else:
                    grouped = xt[b, g][:, pair * PAIR * PACK : (pair + 1) * PAIR * PACK]
                    plane = grouped.rearrange("p (n t) -> p t n", t=PACK)[:, t]
                nc.tensor.matmul(
                    scores[b][:, pair * PAIR : (pair + 1) * PAIR],
                    lhsT=wi_sb[:, g, t : t + 1].to_broadcast([P, P]),
                    rhs=plane,
                    start=(g == 0 and t == 0),
                    stop=(g == PASSES - 1 and t == PACK - 1),
                )

        def score_max(b):
            neg_max[b] = kept("neg_max_%d" % b, [P, 1], F32)
            nc.vector.tensor_reduce(
                out=neg_max[b][:], in_=scores[b][:], axis=mybir.AxisListType.X, op=ALU.max, negate=True
            )

        def score_exp(b):
            expo[b] = kept("expo_%d" % b, [P, N], F32)
            total[b] = kept("total_%d" % b, [P, 1], F32)
            nc.scalar.activation(
                out=expo[b][:], in_=scores[b][:], func=ACT.Exp, bias=neg_max[b][:], scale=1.0, accum_out=total[b][:]
            )

        def invert_total(b):
            inv_total[b] = kept("inv_total_%d" % b, [P, 1], F32)
            nc.vector.reciprocal(out=inv_total[b][:], in_=total[b][:])

        def grouped_tile():
            return ring.tile([P, BANK * PACK], BF16, name="grouped", tag="grouped", bufs=3, align_bytes=64)

        def paced_tile():
            return ring.tile([P, BANK * PACK], BF16, name="paced", tag="paced", bufs=1, align_bytes=64)

        def group_channels(copy, rows, grouped):
            copy(
                out=grouped[:].rearrange("p (t q r j) -> p q j r t", t=PACK, r=2, j=PACK),
                in_=rows[:].rearrange("p j (q r t) -> p q j r t", r=2, t=PACK),
            )
            return grouped

        def move_on_gpsimd(dst, src):
            nc.gpsimd.tensor_scalar(out=dst, in0=src, scalar1=1.0, scalar2=0.0, op0=ALU.mult, op1=ALU.add)

        def group_channels_on_gpsimd(rows):
            grouped = paced_tile()
            move_on_gpsimd(
                grouped[:].rearrange("p (t m j) -> p t m j", t=PACK, j=PACK),
                rows[:].rearrange("p j (m t) -> p t m j", t=PACK),
            )
            return grouped

        def plane_tile():
            return ring.tile([P, PACK, BANK], BF16, name="planes", tag="planes", bufs=3, align_bytes=64)

        def widen_wo(g, h, planes, slots):
            for t in slots:
                first = t * F + h * BANK
                nc.scalar.activation(
                    out=planes[:, t, :],
                    in_=wo_raw[g][:, first : first + BANK].bitcast(FP8),
                    func=ACT.Copy,
                    scale=wo_scale_sb[:, g, t : t + 1],
                )
            return planes

        def group_planes_on_scalar(planes):
            grouped = grouped_tile()
            nc.scalar.copy(
                out=grouped[:].rearrange("p (c i t) -> p c t i", i=4, t=PACK),
                in_=planes[:].rearrange("p t (c i) -> p c t i", i=4),
            )
            return grouped

        def group_planes_on_gpsimd(planes):
            grouped = paced_tile()
            move_on_gpsimd(grouped[:].rearrange("p (n t) -> p n t", t=PACK), planes[:].rearrange("p t n -> p n t"))
            return grouped

        def two_banks_at_a_time(items, multiply, empty):
            for first in range(0, len(items), 2):
                both = items[first : first + 2]
                banks = [multiply(item) for item in both]
                for item, acc in reversed(list(zip(both, banks))):
                    empty(item, acc)

        def pool_keys(b, h, slots):
            if b not in cv:
                cv[b] = kept("cv_%d" % b, [P, 2 * PACK], F32)

            def multiply(t):
                keys = bank()
                mx_product(keys[:], wkq[h], slice(t * P, (t + 1) * P), xq[b], every)
                return keys

            def empty(t, keys):
                col = h * PACK + t
                nc.vector.scalar_tensor_tensor(
                    out=result[b, t][:, h * BANK : (h + 1) * BANK],
                    in0=keys[:],
                    scalar=inv_total[b][:],
                    in1=expo[b][:],
                    op0=ALU.mult,
                    op1=ALU.mult,
                    accum_out=cv[b][:, col : col + 1],
                )

            two_banks_at_a_time(slots, multiply, empty)

        def gate_values(b, h, tiles):
            if (b, h) not in zt:
                zt[b, h] = kept("zt_%d%d" % (b, h), [P, N * PACK], BF16)

            def multiply(j):
                values = bank()
                for t in range(PACK):
                    cols = slice(t * P, (t + 1) * P)
                    mx_product(values[:, cols], wvq[h], cols, xq[b], slice(j * P, (j + 1) * P))
                return values

            def empty(j, values):
                nc.vector.scalar_tensor_tensor(
                    out=zt[b, h][:, j * BANK : (j + 1) * BANK].rearrange("p (n t) -> p n t", t=PACK),
                    in0=values[:].rearrange("p (t n) -> p n t", t=PACK),
                    scalar=0.0,
                    in1=cv[b][:, h * PACK : (h + 1) * PACK].unsqueeze(1).to_broadcast([P, P, PACK]),
                    op0=ALU.max,
                    op1=ALU.mult,
                )

            two_banks_at_a_time(tiles, multiply, empty)

        def gate_values_on_scalar(b, h):
            planes = plane_tile()
            rectified = kept("rectified", [P, PACK * N], F32)
            for t in range(PACK):
                values = bank()
                mx_product(values[:], wvq[h], slice(t * P, (t + 1) * P), xq[b], every)
                nc.scalar.activation(out=rectified[:, t * N : (t + 1) * N], in_=values[:], func=ACT.Relu)
            for t in range(PACK):
                col = h * PACK + t
                nc.scalar.activation(
                    out=planes[:, t, :],
                    in_=rectified[:, t * N : (t + 1) * N],
                    func=ACT.Copy,
                    scale=cv[b][:, col : col + 1],
                )
            return planes

        def project(b, pieces):
            def multiply(piece):
                j, h = piece
                acc = bank()
                mx_product(acc[:], zq[b], slice(j * P, (j + 1) * P), woq[h], every)
                return acc

            def empty(piece, acc):
                j, h = piece
                cols = slice(h * BANK, (h + 1) * BANK)
                nc.vector.tensor_tensor(out=result[b, j][:, cols], in0=acc[:], in1=bias[:, cols], op=ALU.add)

            two_banks_at_a_time(pieces, multiply, empty)

        def store(b, j, cols):
            dst = out[b].rearrange("(p j) f -> p j f", j=TILES)[:, j, cols]
            nc.sync.dma_start(out=dst, in_=result[b, j][:, cols])

        def project_half(b, h, tiles):
            project(b, [(j, h) for j in tiles])
            for j in reversed(tiles):
                store(b, j, slice(h * BANK, (h + 1) * BANK))

        def project_rows(b, j):
            project(b, [(j, 0), (j, 1)])
            store(b, j, slice(0, F))

        on_vector, on_scalar = nc.vector.tensor_copy, nc.scalar.copy
        all_four, first_two, last_two = range(4), range(0, 2), range(2, 4)
        first_pair, second_pair = slice(0, PAIR), slice(PAIR, N)

        turn_x(0, 0, False)
        score(0, 0, 0)
        k00 = group_channels(on_vector, wk_rows[0, 0], grouped_tile())
        quantize_x(0, 0, first_pair)
        quantize(wkq[0][0], k00)
        quantize_x(0, 1, first_pair)
        turn_x(0, 1, False)
        score(0, 0, 1)
        score(0, 1, 0)
        score(0, 1, 1)
        k10 = group_channels(on_vector, wk_rows[1, 0], grouped_tile())
        quantize_x(0, 0, second_pair)
        quantize(wkq[0][1], k10)
        quantize_x(0, 1, second_pair)
        k01 = group_channels(on_scalar, wk_rows[0, 1], grouped_tile())
        k11 = group_channels(on_vector, wk_rows[1, 1], paced_tile())
        o00_planes = widen_wo(0, 0, plane_tile(), first_two)
        score_max(0)
        score_exp(0)
        widen_wo(0, 0, o00_planes, last_two)
        quantize(wkq[1][0], k01)
        quantize(wkq[1][1], k11)
        invert_total(0)

        v00 = group_channels_on_gpsimd(wv_rows[0, 0])
        pool_keys(0, 0, all_four)
        turn_x(1, 0, True)
        turn_x(1, 1, True)
        pool_keys(0, 1, all_four)
        for g in range(PASSES):
            quantize_x(1, g, every)
        for pair in range(2):
            for g in range(PASSES):
                score(1, pair, g)
        v10 = group_channels(on_scalar, wv_rows[1, 0], grouped_tile())
        score_max(1)
        score_exp(1)
        quantize(wvq[0][1], v10)
        quantize(wvq[0][0], v00)
        invert_total(1)

        v11 = group_channels_on_gpsimd(wv_rows[1, 1])
        v01 = group_channels(on_scalar, wv_rows[0, 1], grouped_tile())
        pool_keys(1, 0, all_four)
        pool_keys(1, 1, first_two)
        quantize(wvq[1][0], v01)
        quantize(wvq[1][1], v11)

        o00 = group_planes_on_gpsimd(o00_planes)
        o10_planes = widen_wo(1, 0, plane_tile(), all_four)
        o01_planes = widen_wo(0, 1, plane_tile(), all_four)
        pool_keys(1, 1, last_two)
        gate_values(0, 0, all_four)
        quantize(woq[0][0], o00)
        o10 = group_planes_on_gpsimd(o10_planes)
        o01 = group_planes_on_scalar(o01_planes)
        o11_planes = widen_wo(1, 1, plane_tile(), all_four)
        gate_values(0, 1, all_four)
        gate_values(1, 0, first_two)
        z11 = group_planes_on_scalar(gate_values_on_scalar(1, 1))
        quantize(zq[0][0], zt[0, 0])
        quantize(zq[0][1], zt[0, 1])
        quantize(woq[1][0], o01)
        quantize(woq[0][1], o10)

        o11 = group_planes_on_gpsimd(o11_planes)
        gate_values(1, 0, last_two)
        project_half(0, 0, first_two)
        project_half(0, 0, last_two)
        quantize(woq[1][1], o11)
        quantize(zq[1][0], zt[1, 0])
        quantize(zq[1][1], z11)
        project_half(0, 1, first_two)
        project_half(0, 1, last_two)
        for j in range(TILES - 1):
            project_rows(1, j)
        for h in range(2):
            project_half(1, h, range(TILES - 1, TILES))
